import numpy as np
import ml_dtypes


def mxq(x, axis, fmt="e4m3"):
    dtype, down = {"e4m3": (ml_dtypes.float8_e4m3fn, 7), "e5m2": (ml_dtypes.float8_e5m2, 14)}[fmt]
    v = np.moveaxis(np.asarray(x, np.float32).astype(ml_dtypes.bfloat16).astype(np.float64), axis, -1)
    blocks = v.reshape(v.shape[:-1] + (-1, 32))
    amax = np.abs(blocks).max(-1, keepdims=True)
    byte = np.maximum(np.where(amax > 0, np.frexp(amax)[1] - 1 + 127, 0) - down, 1)
    scale = np.exp2(byte - 127.0)
    codes = (blocks / scale).astype(np.float32).astype(dtype).astype(np.float64)
    return np.moveaxis((codes * scale).reshape(v.shape), -1, axis)


WIDE = False


def mx_kscale(k):
    if not WIDE:
        return np.ones(k)
    levels = np.array([10, -10, 5, -5, 0])
    if k % 512:
        return np.exp2(np.random.permutation(np.resize(levels, k // 32))).repeat(32)
    a = np.empty((k // 512, 16))
    for p in range(k // 512):
        a[p, :8] = np.random.permutation(np.resize(levels, 8))
        for g in range(8):
            far = levels[np.abs(levels - a[p, g]) >= 10]
            a[p, g + 8] = far[np.random.randint(len(far))]
    return np.exp2(a.ravel()).repeat(32)


BF16 = ml_dtypes.bfloat16


def bf(x):
    return np.asarray(x, np.float32).astype(BF16)


def f64(x):
    return np.asarray(x).astype(np.float64)


E2M1 = np.array([0.0, 0.5, 1.0, 1.5, 2.0, 3.0, 4.0, 6.0, -0.0, -0.5, -1.0, -1.5, -2.0, -3.0, -4.0, -6.0])


def pack_weight(w, fmt):
    k, n = w.shape
    w = f64(bf(w)).reshape(k // 32, 32, n)
    amax = np.abs(w).max(1)
    if fmt == "e4m3":
        byte = np.frexp(amax)[1] - 1 + 127 - 7
    else:
        mant, ex = np.frexp(amax / 6.0)
        byte = np.where(mant > 0.5, ex, ex - 1) + 127
    byte = np.clip(np.where(amax > 0, byte, 1), 1, 254)
    scaled = (w * np.exp2(127.0 - byte)[:, None, :]).reshape(k, n).astype(np.float32)
    by_word = np.ascontiguousarray(scaled.reshape(k // 512, 128, 4, n).transpose(0, 1, 3, 2))
    if fmt == "e4m3":
        words = by_word.astype(ml_dtypes.float8_e4m3fn).view(np.uint8)
    else:
        c = by_word.astype(ml_dtypes.float4_e2m1fn).view(np.uint8) & 0xF
        words = c[..., 0::2] | (c[..., 1::2] << 4)
    return np.ascontiguousarray(words), np.ascontiguousarray(byte.astype(np.uint8).reshape(k // 512, 16, n))


def unpack_weight(words, scales, fmt):
    g, p, n, _ = words.shape
    if fmt == "e4m3":
        vals = np.ascontiguousarray(words).view(ml_dtypes.float8_e4m3fn).astype(np.float64)
    else:
        nib = np.empty((g, p, n, 4), np.uint8)
        nib[..., 0::2] = words & 0xF
        nib[..., 1::2] = words >> 4
        vals = E2M1[nib]
    vals = vals * np.repeat(np.exp2(scales.astype(np.float64) - 127.0), 8, axis=1)[..., None]
    return vals.transpose(0, 1, 3, 2).reshape(g * 512, n)
def pack4(w):
    words, scales = pack_weight(w, "e2m1")
    return words.reshape(words.shape[0], 128, -1), scales


def unpack4(words, scales):
    return unpack_weight(words.reshape(words.shape[0], 128, -1, 2), scales, "e2m1")


def planes(Y):
    n, m = Y.shape
    b = f64(bf(Y)).reshape(n // 32, 32, m)
    amax = np.abs(b).max(1)
    byte = np.clip(np.where(amax > 0, np.frexp(amax)[1] - 1 + 127 - 7, 1), 1, 254)
    codes = (b * np.exp2(127.0 - byte)[:, None, :]).reshape(n, m).astype(np.float32).astype(ml_dtypes.float8_e4m3fn).view(np.uint8)
    words = codes.reshape(n // 512, 128, 4, m).transpose(0, 1, 3, 2)
    return np.ascontiguousarray(words), np.ascontiguousarray(byte.astype(np.uint8).reshape(n // 512, 16, m))


B, P, S, K, C = 2, 1024, 512, 1024, 512


def instance_norm(x):
    mu = np.mean(x, axis=1, keepdims=True)
    centered = x - mu
    var = np.mean(centered * centered, axis=1, keepdims=True)
    return centered / np.sqrt(var + 1e-5)


def setup_inputs():
    s, t = mx_kscale(S), mx_kscale(K)
    x = bf(0.5 + 1.5 * np.random.standard_normal((B, P, C)))
    m = bf(np.random.standard_normal((B, P, S)) * s)
    wm_words, wm_scales = pack4(np.random.standard_normal((S, K)) / np.sqrt(S) / s[:, None])
    bm = bf(0.3 * np.random.standard_normal(K))
    g = bf(np.random.standard_normal(K) * t)
    wg_words, wg_scales = pack4(np.random.standard_normal((K, C)) / np.sqrt(K) / t[:, None])
    wb_words, wb_scales = pack4(np.random.standard_normal((K, C)) / np.sqrt(K) / t[:, None])
    return {
        "x": x,
        "m": m,
        "wm_words": wm_words,
        "wm_scales": wm_scales,
        "bm": bm,
        "g": g,
        "wg_words": wg_words,
        "wg_scales": wg_scales,
        "wb_words": wb_words,
        "wb_scales": wb_scales,
    }


def core(x, m, wm_words, wm_scales, bm, g, wg_words, wg_scales, wb_words, wb_scales):
    h = (mxq(f64(m), 2, "e4m3") @ unpack4(wm_words, wm_scales)) + f64(bm)[None, None, :]
    a = np.maximum(h, 0.0) * f64(g)[None, None, :]
    aq = mxq(a, 2, "e4m3")
    gamma = aq @ unpack4(wg_words, wg_scales)
    beta = aq @ unpack4(wb_words, wb_scales)
    xn = instance_norm(f64(x))
    y = xn * (1.0 + gamma) + beta
    return np.where(y >= 0.0, y, 0.2 * y)


def reference(x, m, wm_words, wm_scales, bm, g, wg_words, wg_scales, wb_words, wb_scales):
    R_out = core(x, m, wm_words, wm_scales, bm, g, wg_words, wg_scales, wb_words, wb_scales)
    words, scales = planes(np.moveaxis(R_out, 2, 0).reshape(512, -1))
    return R_out, words, scales

@@ -1,0 +1,375 @@
+from contextlib import ExitStack
+
+import concourse.mybir as mybir
+from concourse.masks import make_identity
+
+B, POS, S, K, C = 2, 1024, 512, 1024, 512
+FLOPS = 3 * 2 * B * POS * S * K
+
+F32 = mybir.dt.float32
+BF16 = mybir.dt.bfloat16
+I32 = mybir.dt.int32
+U32 = mybir.dt.uint32
+U8 = mybir.dt.uint8
+FP8X4 = mybir.dt.float8_e4m3fn_x4
+FP4X4 = mybir.dt.float4_e2m1fn_x4
+ACT = mybir.ActivationFunctionType
+ALU = mybir.AluOpType
+
+P = 128
+R = 512
+NCH = B * POS // R
+EPS = 1e-5
+ACT_INTERLEAVE = (1, 3, 5, 7)
+
+
+def tile_spademodulationpointwise_x2_kernel(
+    tc, x, m, wm_words, wm_scales, bm, g, wg_words, wg_scales, wb_words, wb_scales, out_0, out_1, out_2
+):
+    nc = tc.nc
+    with ExitStack() as ctx:
+        keep = ctx.enter_context(tc.tile_pool(name="keep", bufs=1))
+        work = ctx.enter_context(tc.tile_pool(name="work", bufs=2))
+        psum = ctx.enter_context(tc.psum_pool(name="psum", bufs=2))
+
+        def fixed(name, shape, dtype):
+            return keep.tile(shape, dtype, name=name, tag=name, align_bytes=64)
+
+        def turn(tag, shape, dtype, bufs):
+            return work.tile(shape, dtype, name=tag, tag=tag, bufs=bufs, align_bytes=64)
+
+        ident = fixed("ident", [P, P], F32)
+        m_raw = [fixed("m_raw%d" % q, [P, 4, S], BF16) for q in range(NCH)]
+        x_raw = [fixed("x_raw%d" % q, [P, 4, C], BF16) for q in range(NCH)]
+        wm_raw = fixed("wm_raw", [P, 2 * K], U8)
+        wm_cols = fixed("wm_cols", [P, 2, 4, 256], U8)
+        wms_raw = fixed("wms_raw", [P, K], U8)
+        wms_cols = fixed("wms_cols", [P, 2, 4, P], U8)
+        w2_raw = fixed("w2_raw", [P, 2, 2, 2 * C], U8)
+        w2_cols = fixed("w2_cols", [P, 2, 2, 4, 256], U8)
+        w2s_raw = fixed("w2s_raw", [P, 2, 2, C], U8)
+        w2s_cols = fixed("w2s_cols", [P, 2, 2, 4, P], U8)
+        bm_sb = fixed("bm_sb", [P, 2, 4], BF16)
+        g_sb = fixed("g_sb", [P, 2, 4], BF16)
+        g_abs = fixed("g_abs", [P, 2, 4], F32)
+        g_sgn = fixed("g_sgn", [P, 2, 4], F32)
+        g_bias = fixed("g_bias", [P, 2, 4], F32)
+        neg_half = fixed("neg_half", [P, 4], F32)
+
+        nc.vector.memset(wms_raw[:].bitcast(I32), 0)
+        nc.gpsimd.memset(w2s_raw[:].rearrange("p a k n -> p (a k n)").bitcast(I32), 0)
+        nc.gpsimd.memset(neg_half[:], -0.5)
+        make_identity(nc, ident[:])
+
+        def rows(q):
+            return q // 2, (q % 2) * R
+
+        def load_m(q):
+            b, r0 = rows(q)
+            for h in range(2):
+                src = m[b, r0 + 256 * h : r0 + 256 * (h + 1), :].rearrange("(a p) s -> p a s", p=P)
+                nc.sync.dma_start(out=m_raw[q][:, 2 * h : 2 * h + 2, :], in_=src)
+
+        def load_x(q):
+            b, r0 = rows(q)
+            src = x[b, r0 : r0 + R, :].rearrange("(a p) s -> p a s", p=P)
+            nc.sync.dma_start(out=x_raw[q][:], in_=src)
+
+        load_m(0)
+        nc.sync.dma_start(out=wm_raw[:].bitcast(I32), in_=wm_words[0].bitcast(I32))
+        nc.scalar.dma_start(out=g_sb[:], in_=g.rearrange("(g p t) -> p g t", p=P, t=4))
+        nc.scalar.dma_start(out=bm_sb[:], in_=bm.rearrange("(g p t) -> p g t", p=P, t=4))
+        for Q in range(4):
+            nc.scalar.dma_start(
+                out=wms_raw[32 * Q : 32 * Q + 4, :].bitcast(I32), in_=wm_scales[0, 4 * Q : 4 * Q + 4, :].bitcast(I32)
+            )
+        load_x(0)
+        load_x(1)
+        for w, words in enumerate((wg_words, wb_words)):
+            nc.sync.dma_start(out=w2_raw[:, w, :, :].bitcast(I32), in_=words.rearrange("k p n -> p k n").bitcast(I32))
+        for w, scales in enumerate((wg_scales, wb_scales)):
+            for Q in range(4):
+                nc.sync.dma_start(
+                    out=w2s_raw[32 * Q : 32 * Q + 4, w, :, :].bitcast(I32),
+                    in_=scales[:, 4 * Q : 4 * Q + 4, :].rearrange("k q n -> q k n").bitcast(I32),
+                )
+        load_m(1)
+        load_m(2)
+        load_x(2)
+        load_x(3)
+        load_m(3)
+
+        mg, mq, ms = {}, {}, {}
+        planar, grouped, aq, asc = {}, {}, {}, {}
+        s1_ps = {}
+        xt, xn = {}, {}
+        stats = [fixed("stats%d" % b, [P, 4, 2, 6], F32) for b in range(B)]
+        mv = [fixed("mv%d" % b, [P, 4, 2], F32) for b in range(B)]
+        rs = [fixed("rs%d" % b, [P, 4], F32) for b in range(B)]
+        gam, bet, u_t, y_t, o_t = {}, {}, {}, {}, {}
+        ob, oq, osc = {}, {}, {}
+
+        def prep_gain():
+            flat = "p g t -> p (g t)"
+            gf = g_sb[:].rearrange(flat)
+            nc.vector.scalar_tensor_tensor(
+                out=g_abs[:].rearrange(flat), in0=gf, scalar=-1.0, in1=gf, op0=ALU.mult, op1=ALU.max
+            )
+            nc.vector.tensor_scalar(g_sgn[:].rearrange(flat), gf, 0.0, 2.0, op0=ALU.is_ge, op1=ALU.mult)
+            nc.vector.tensor_tensor(
+                out=g_bias[:].rearrange(flat), in0=g_abs[:].rearrange(flat), in1=bm_sb[:].rearrange(flat), op=ALU.mult
+            )
+            nc.vector.tensor_scalar_add(g_sgn[:].rearrange(flat), g_sgn[:].rearrange(flat), -1.0)
+
+        def perm_wm(k):
+            src = wm_raw[:].rearrange("p (k c t b) -> p k t c b", k=2, t=4, b=2)
+            nc.vector.tensor_copy(
+                out=wm_cols[:, k, :, :].rearrange("p t (c b) -> p t c b", b=2), in_=src[:, k, :, :, :]
+            )
+
+        def perm_wms():
+            nc.vector.tensor_copy(
+                out=wms_cols[:], in_=wms_raw[:].rearrange("p (k c t) -> p k t c", k=2, t=4)
+            )
+
+        def perm_w2(w, k):
+            nc.vector.tensor_copy(
+                out=w2_cols[:, w, k, :, :].rearrange("p t (c b) -> p t c b", b=2),
+                in_=w2_raw[:, w, k, :].rearrange("p (c t b) -> p t c b", t=4, b=2),
+            )
+
+        def perm_w2s(w):
+            nc.vector.tensor_copy(
+                out=w2s_cols[:, w, :, :, :], in_=w2s_raw[:, w, :, :].rearrange("p k (c t) -> p k t c", t=4)
+            )
+
+        def m_turn(q, h):
+            pt = psum.tile([P, 2, 2, P], F32, name="pt", tag="pt", bufs=2)
+            for a in range(2):
+                words = m_raw[q][:, 2 * h + a, :].bitcast(F32)
+                for u in range(2):
+                    nc.tensor.transpose(pt[:, a, u, :], words[:, u : 2 * P : 2], ident[:])
+            if h == 0:
+                mg[q] = turn("mg", [P, R, 4], BF16, 2)
+            dst = mg[q][:, 256 * h : 256 * (h + 1), :].rearrange("p r t -> p (r t)").bitcast(F32)
+            nc.scalar.copy(
+                out=dst.rearrange("p (a r u) -> p a r u", a=2, u=2), in_=pt[:].rearrange("p a u r -> p a r u")
+            )
+
+        def m_quant(q):
+            mq[q] = turn("mq", [P, R], U32, 2)
+            ms[q] = turn("ms", [P, R], U8, 2)
+            nc.vector.quantize_mx(
+                out=mq[q][:].bitcast(FP8X4), scales=ms[q][:], in_=mg[q][:].rearrange("p r t -> p (r t)")
+            )
+
+        def x_turn(q, h):
+            pt = psum.tile([P, 2, 2, P], F32, name="pt", tag="pt", bufs=2)
+            for a in range(2):
+                words = x_raw[q][:, 2 * h + a, :].bitcast(F32)
+                for u in range(2):
+                    nc.tensor.transpose(pt[:, a, u, :], words[:, u : 2 * P : 2], ident[:])
+            if h == 0:
+                xt[q] = turn("xt", [P, 2, R], F32, 4)
+            nc.scalar.copy(
+                out=xt[q][:, :, 256 * h : 256 * (h + 1)].rearrange("p u (a r) -> p u a r", a=2),
+                in_=pt[:].rearrange("p a u r -> p u a r"),
+            )
+
+        def x_of(q, t):
+            return xt[q][:, t // 2, :].bitcast(BF16)[:, t % 2 : 2 * R : 2]
+
+        def x_stats(q, t):
+            nc.vector.bn_stats(out=stats[q // 2][:, t, q % 2, :], in_=x_of(q, t))
+
+        def x_aggr(b):
+            for t in range(4):
+                nc.vector.bn_aggr(out=mv[b][:, t, :], in_=stats[b][:, t, :, :].rearrange("p c k -> p (c k)"))
+            nc.gpsimd.tensor_scalar(rs[b][:], mv[b][:, :, 1], EPS, 1.0, op0=ALU.add, op1=ALU.mult)
+            nc.gpsimd.tensor_tensor(out=rs[b][:], in0=rs[b][:], in1=neg_half[:], op=ALU.pow)
+
+        def x_norm(q):
+            b = q // 2
+            xn[q] = turn("xn", [P, 4, R], F32, 4)
+            for t in range(4):
+                nc.vector.tensor_scalar(
+                    xn[q][:, t, :], x_of(q, t), mv[b][:, t, 0:1], rs[b][:, t : t + 1], op0=ALU.subtract, op1=ALU.mult
+                )
+
+        def stage1(q, j):
+            k = j // 2
+            for t in (2 * (j % 2), 2 * (j % 2) + 1):
+                ps = psum.tile([P, R], F32, name="ps1", tag="ps1", bufs=2)
+                nc.tensor.matmul_mx(
+                    out=ps[:], lhsT=wm_cols[:, k, t, :].bitcast(FP4X4), lhsT_scale=wms_cols[:, k, t, :],
+                    rhs=mq[q][:].bitcast(FP8X4), rhs_scale=ms[q][:], start=True, stop=True,
+                )
+                s1_ps[q, k, t] = ps
+
+        def relu(q, j):
+            k = j // 2
+            if j % 2 == 0:
+                planar[q, k] = turn("planar", [P, 4, R], BF16, 3)
+            for t in (2 * (j % 2), 2 * (j % 2) + 1):
+                nc.scalar.activation(
+                    out=planar[q, k][:, t, :], in_=s1_ps[q, k, t][:], func=ACT.Relu,
+                    scale=g_abs[:, k, t : t + 1], bias=g_bias[:, k, t : t + 1],
+                )
+
+        def sign(q, j):
+            k = j // 2
+            for t in (2 * (j % 2), 2 * (j % 2) + 1):
+                nc.vector.tensor_scalar_mul(planar[q, k][:, t, :], planar[q, k][:, t, :], g_sgn[:, k, t : t + 1])
+
+        def interleave(q, k):
+            grouped[q, k] = turn("grouped", [P, R, 4], BF16, 2)
+            op = nc.scalar.copy if 2 * q + k in ACT_INTERLEAVE else nc.vector.tensor_copy
+            op(out=grouped[q, k][:], in_=planar[q, k][:].rearrange("p t r -> p r t"))
+
+        def a_quant(q, k):
+            aq[q, k] = turn("aq", [P, R], U32, 4)
+            asc[q, k] = turn("asc", [P, R], U8, 4)
+            nc.vector.quantize_mx(
+                out=aq[q, k][:].bitcast(FP8X4), scales=asc[q, k][:], in_=grouped[q, k][:].rearrange("p r t -> p (r t)")
+            )
+
+        def stage2(q, t):
+            for w, store in ((0, gam), (1, bet)):
+                ps = psum.tile([P, R], F32, name="ps2", tag="ps2", bufs=4)
+                for k in range(2):
+                    nc.tensor.matmul_mx(
+                        out=ps[:], lhsT=w2_cols[:, w, k, t, :].bitcast(FP4X4), lhsT_scale=w2s_cols[:, w, k, t, :],
+                        rhs=aq[q, k][:].bitcast(FP8X4), rhs_scale=asc[q, k][:], start=(k == 0), stop=(k == 1),
+                    )
+                store[q, t] = ps
+
+        def mod_u(q, t):
+            u_t[q, t] = turn("u", [P, R], F32, 3)
+            nc.vector.scalar_tensor_tensor(
+                out=u_t[q, t][:], in0=gam[q, t][:], scalar=1.0, in1=xn[q][:, t, :], op0=ALU.add, op1=ALU.mult
+            )
+
+        def mod_y(q, t):
+            y_t[q, t] = turn("y", [P, R], F32, 3)
+            nc.vector.tensor_tensor(out=y_t[q, t][:], in0=bet[q, t][:], in1=u_t[q, t][:], op=ALU.add)
+
+        def mod_o(q, t):
+            if t == 0:
+                o_t[q] = turn("o", [P, 4, R], F32, 2)
+            yy = y_t[q, t][:]
+            nc.vector.scalar_tensor_tensor(out=o_t[q][:, t, :], in0=yy, scalar=0.2, in1=yy, op0=ALU.mult, op1=ALU.max)
+
+        def out_turn(q, a):
+            pt = psum.tile([P, 4, P], F32, name="pt", tag="pt", bufs=2)
+            for t in range(4):
+                nc.tensor.transpose(pt[:, t, :], o_t[q][:, t, P * a : P * (a + 1)], ident[:])
+            orow = turn("orow", [P, P, 4], F32, 3)
+            nc.scalar.copy(out=orow[:], in_=pt[:].rearrange("r t p -> r p t"))
+            b, r0 = rows(q)
+            nc.sync.dma_start(
+                out=out_0[b, r0 + P * a : r0 + P * (a + 1), :], in_=orow[:].rearrange("r p t -> r (p t)")
+            )
+
+        def out_cast(q, h):
+            if h == 0:
+                ob[q] = turn("ob", [P, R, 4], BF16, 2)
+            nc.scalar.copy(
+                out=ob[q][:, 256 * h : 256 * (h + 1), :],
+                in_=o_t[q][:, :, 256 * h : 256 * (h + 1)].rearrange("p t r -> p r t"),
+            )
+
+        def out_quant(q, h):
+            if h == 0:
+                oq[q] = turn("oq", [P, R], U32, 2)
+                osc[q] = turn("osc", [P, R], U8, 2)
+            part = slice(256 * h, 256 * (h + 1))
+            nc.vector.quantize_mx(
+                out=oq[q][:, part].bitcast(FP8X4), scales=osc[q][:, part],
+                in_=ob[q][:, part, :].rearrange("p r t -> p (r t)"),
+            )
+            c0 = q * R + 256 * h
+            nc.sync.dma_start(
+                out=out_1[0].rearrange("p n t -> p (n t)")[:, 4 * c0 : 4 * (c0 + 256)].bitcast(I32),
+                in_=oq[q][:, part].bitcast(I32),
+            )
+            if h == 1:
+                for Q in range(4):
+                    nc.sync.dma_start(
+                        out=out_2[0, 4 * Q : 4 * Q + 4, q * R : (q + 1) * R].bitcast(I32),
+                        in_=osc[q][32 * Q : 32 * Q + 4, :].bitcast(I32),
+                    )
+
+        with tc.manual_schedule():
+            perm_wms()
+            perm_wm(0)
+            prep_gain()
+            perm_wm(1)
+            for i in range(-8, 4 * NCH + 9):
+                qc, tcur = divmod(i, 4)
+                if 0 <= qc < NCH:
+                    stage2(qc, tcur)
+                qb, jb = divmod(i + 6, 4)
+                if 0 <= qb < NCH:
+                    stage1(qb, jb)
+                    relu(qb, jb)
+                if 0 <= qc < NCH:
+                    mod_u(qc, tcur)
+                qs, js = divmod(i + 5, 4)
+                if 0 <= qs < NCH:
+                    sign(qs, js)
+                if 0 <= qc < NCH:
+                    mod_y(qc, tcur)
+                if i % 2 == 0:
+                    qi, ki = divmod((i + 4) // 2, 2)
+                    if 0 <= qi < NCH:
+                        interleave(qi, ki)
+                else:
+                    qi, ki = divmod((i + 3) // 2, 2)
+                    if 0 <= qi < NCH:
+                        a_quant(qi, ki)
+                if i in (-4, -3):
+                    perm_w2s(i + 4)
+                if i in (-4, -3):
+                    perm_w2(0, i + 4)
+                if i in (-2, -1):
+                    perm_w2(1, i + 2)
+                qa, ha = divmod(i + 8, 4)
+                if 0 <= qa < NCH and ha < 2:
+                    m_turn(qa, ha)
+                    if ha == 1:
+                        m_quant(qa)
+                if i == -6:
+                    x_turn(0, 0)
+                    x_turn(0, 1)
+                if i == -5:
+                    x_turn(1, 0)
+                    x_turn(1, 1)
+                    for t in range(4):
+                        x_stats(0, t)
+                if i == -4:
+                    for t in range(4):
+                        x_stats(1, t)
+                    x_aggr(0)
+                if i == -3:
+                    x_norm(0)
+                if i == 0:
+                    x_norm(1)
+                if 0 <= i < 4:
+                    x_turn(2 + i // 2, i % 2)
+                if i in (2, 3, 4, 5):
+                    for t in (0, 1):
+                        x_stats(2 + (i - 2) // 2, 2 * (i % 2) + t)
+                if i == 5:
+                    x_aggr(1)
+                    x_norm(2)
+                if i == 7:
+                    x_norm(3)
+                if 0 <= qc < NCH:
+                    mod_o(qc, tcur)
+                qd, ad = divmod(i - 5, 4)
+                if 0 <= qd < NCH:
+                    out_turn(qd, ad)
+                    if ad < 2:
+                        out_cast(qd, ad)
+                    if ad in (1, 2):
+                        out_quant(qd, ad - 1)

@@ -18,9 +18,17 @@ ALU = mybir.AluOpType
 
 P = 128
 R = 512
-NCH = B * POS // R
+CHUNKS = B * POS // R
+LAST = CHUNKS - 1
+KG = K // 512
 EPS = 1e-5
-ACT_INTERLEAVE = (1, 3, 5, 7)
+LEAK = 0.2
+HALVES = (slice(0, R // 2), slice(R // 2, R))
+
+SCALAR_GROUPS = (
+    (0, 0, 0), (0, 0, 1), (0, 1, 1), (1, 0, 0), (1, 1, 1), (2, 0, 0), (2, 0, 1), (2, 1, 0), (3, 0, 0),
+    (3, 0, 1), (3, 1, 0),
+)
 
 
 def tile_spademodulationpointwise_x2_kernel(
@@ -38,51 +46,69 @@ def tile_spademodulationpointwise_x2_kernel(
         def turn(tag, shape, dtype, bufs):
             return work.tile(shape, dtype, name=tag, tag=tag, bufs=bufs, align_bytes=64)
 
-        ident = fixed("ident", [P, P], F32)
-        m_raw = [fixed("m_raw%d" % q, [P, 4, S], BF16) for q in range(NCH)]
-        x_raw = [fixed("x_raw%d" % q, [P, 4, C], BF16) for q in range(NCH)]
-        wm_raw = fixed("wm_raw", [P, 2 * K], U8)
-        wm_cols = fixed("wm_cols", [P, 2, 4, 256], U8)
-        wms_raw = fixed("wms_raw", [P, K], U8)
-        wms_cols = fixed("wms_cols", [P, 2, 4, P], U8)
-        w2_raw = fixed("w2_raw", [P, 2, 2, 2 * C], U8)
-        w2_cols = fixed("w2_cols", [P, 2, 2, 4, 256], U8)
-        w2s_raw = fixed("w2s_raw", [P, 2, 2, C], U8)
-        w2s_cols = fixed("w2s_cols", [P, 2, 2, 4, P], U8)
-        bm_sb = fixed("bm_sb", [P, 2, 4], BF16)
-        g_sb = fixed("g_sb", [P, 2, 4], BF16)
-        g_abs = fixed("g_abs", [P, 2, 4], F32)
-        g_sgn = fixed("g_sgn", [P, 2, 4], F32)
-        g_bias = fixed("g_bias", [P, 2, 4], F32)
-        neg_half = fixed("neg_half", [P, 4], F32)
+        def embed_bank():
+            return psum.tile([P, R], F32, name="embed", tag="embed", bufs=2)
 
-        nc.vector.memset(wms_raw[:].bitcast(I32), 0)
-        nc.gpsimd.memset(w2s_raw[:].rearrange("p a k n -> p (a k n)").bitcast(I32), 0)
-        nc.gpsimd.memset(neg_half[:], -0.5)
+        def map_bank(pieces, width):
+            return psum.tile([P, pieces, width], F32, name="map", tag="map", bufs=3)
+
+        def turn_bank():
+            return psum.tile([P, 4, P], F32, name="turned", tag="turned", bufs=3)
+
+        ident = fixed("ident", [P, P], F32)
+        zero = fixed("zero", [P, 4], F32)
+        neg_half = fixed("neg_half", [P, 4], F32)
+        m_raw = [fixed("m_raw%d" % q, [P, 4, S], BF16) for q in range(CHUNKS)]
+        x_raw = [fixed("x_raw%d" % q, [P, 4, C], BF16) for q in range(CHUNKS)]
+        wm_raw = fixed("wm_raw", [P, KG, 2 * 512], U8)
+        wm_cols = fixed("wm_cols", [P, KG, 4, 2 * P], U8)
+        wm_scales_raw = fixed("wm_scales_raw", [P, KG, 512], U8)
+        wm_scales_cols = fixed("wm_scales_cols", [P, KG, 4, P], U8)
+        w2_raw = fixed("w2_raw", [P, 2, KG, 2 * C], U8)
+        w2_cols = fixed("w2_cols", [P, 2, KG, 4, 2 * P], U8)
+        w2_scales_raw = fixed("w2_scales_raw", [P, 2, KG, C], U8)
+        w2_scales_cols = fixed("w2_scales_cols", [P, 2, KG, 4, P], U8)
+        bm_sb = fixed("bm_sb", [P, KG, 4], BF16)
+        g_sb = fixed("g_sb", [P, KG, 4], BF16)
+        g_abs = fixed("g_abs", [P, KG, 4], F32)
+        g_sign = fixed("g_sign", [P, KG, 4], F32)
+        g_bias = fixed("g_bias", [P, KG, 4], F32)
+        stats = [fixed("stats%d" % b, [P, 2, 4, 6], F32) for b in range(B)]
+        mean_var = [fixed("mean_var%d" % b, [P, 4, 2], F32) for b in range(B)]
+        rstd = [fixed("rstd%d" % b, [P, 4], F32) for b in range(B)]
+        shift = [fixed("shift%d" % b, [P, 4], F32) for b in range(B)]
+
+        o_scales = fixed("o_scales", [P, CHUNKS, R], U8)
+
+        nc.vector.memset(wm_scales_raw[:].rearrange("p k n -> p (k n)").bitcast(I32), 0)
+        nc.vector.memset(w2_scales_raw[:].rearrange("p w k n -> p (w k n)").bitcast(I32), 0)
+        nc.vector.memset(zero[:], 0.0)
         make_identity(nc, ident[:])
 
-        def rows(q):
-            return q // 2, (q % 2) * R
+        def place(q):
+            return q // (POS // R), q % (POS // R) * R
 
         def load_m(q):
-            b, r0 = rows(q)
+            b, r0 = place(q)
             for h in range(2):
-                src = m[b, r0 + 256 * h : r0 + 256 * (h + 1), :].rearrange("(a p) s -> p a s", p=P)
-                nc.sync.dma_start(out=m_raw[q][:, 2 * h : 2 * h + 2, :], in_=src)
+                rows = m[b, r0 + 256 * h : r0 + 256 * (h + 1), :].rearrange("(a p) s -> p a s", p=P)
+                nc.sync.dma_start(out=m_raw[q][:, 2 * h : 2 * h + 2, :], in_=rows)
 
         def load_x(q):
-            b, r0 = rows(q)
-            src = x[b, r0 : r0 + R, :].rearrange("(a p) s -> p a s", p=P)
-            nc.sync.dma_start(out=x_raw[q][:], in_=src)
+            b, r0 = place(q)
+            nc.sync.dma_start(out=x_raw[q][:], in_=x[b, r0 : r0 + R, :].rearrange("(a p) c -> p a c", p=P))
 
+        nc.sync.dma_start(out=wm_raw[:].rearrange("p k n -> p (k n)").bitcast(I32), in_=wm_words[0].bitcast(I32))
         load_m(0)
-        nc.sync.dma_start(out=wm_raw[:].bitcast(I32), in_=wm_words[0].bitcast(I32))
-        nc.scalar.dma_start(out=g_sb[:], in_=g.rearrange("(g p t) -> p g t", p=P, t=4))
-        nc.scalar.dma_start(out=bm_sb[:], in_=bm.rearrange("(g p t) -> p g t", p=P, t=4))
         for Q in range(4):
             nc.scalar.dma_start(
-                out=wms_raw[32 * Q : 32 * Q + 4, :].bitcast(I32), in_=wm_scales[0, 4 * Q : 4 * Q + 4, :].bitcast(I32)
+                out=wm_scales_raw[32 * Q : 32 * Q + 4, :, :].rearrange("p k n -> p (k n)").bitcast(I32),
+                in_=wm_scales[0, 4 * Q : 4 * Q + 4, :].bitcast(I32),
             )
+        nc.scalar.dma_start(out=g_sb[:], in_=g.rearrange("(k p t) -> p k t", p=P, t=4))
+        nc.scalar.dma_start(out=bm_sb[:], in_=bm.rearrange("(k p t) -> p k t", p=P, t=4))
+        nc.scalar.activation(out=neg_half[:], in_=zero[:], func=ACT.Identity, bias=-0.5, scale=1.0)
+        load_m(1)
         load_x(0)
         load_x(1)
         for w, words in enumerate((wg_words, wb_words)):
@@ -90,286 +116,352 @@ def tile_spademodulationpointwise_x2_kernel(
         for w, scales in enumerate((wg_scales, wb_scales)):
             for Q in range(4):
                 nc.sync.dma_start(
-                    out=w2s_raw[32 * Q : 32 * Q + 4, w, :, :].bitcast(I32),
+                    out=w2_scales_raw[32 * Q : 32 * Q + 4, w, :, :].bitcast(I32),
                     in_=scales[:, 4 * Q : 4 * Q + 4, :].rearrange("k q n -> q k n").bitcast(I32),
                 )
-        load_m(1)
         load_m(2)
         load_x(2)
         load_x(3)
         load_m(3)
 
-        mg, mq, ms = {}, {}, {}
-        planar, grouped, aq, asc = {}, {}, {}, {}
-        s1_ps = {}
-        xt, xn = {}, {}
-        stats = [fixed("stats%d" % b, [P, 4, 2, 6], F32) for b in range(B)]
-        mv = [fixed("mv%d" % b, [P, 4, 2], F32) for b in range(B)]
-        rs = [fixed("rs%d" % b, [P, 4], F32) for b in range(B)]
-        gam, bet, u_t, y_t, o_t = {}, {}, {}, {}, {}
-        ob, oq, osc = {}, {}, {}
+        m_turned, m_grouped, m_codes, m_scales = {}, {}, {}, {}
+        h_bank, a_planar, a_grouped, a_codes, a_scales = {}, {}, {}, {}, {}
+        stat_bank, x_bank, xn, map_banks = {}, {}, {}, {}
+        prod, y_tile, o_tile, o_turned = {}, {}, {}, {}
+        o_grouped, o_codes = {}, {}
 
-        def prep_gain():
-            flat = "p g t -> p (g t)"
-            gf = g_sb[:].rearrange(flat)
-            nc.vector.scalar_tensor_tensor(
-                out=g_abs[:].rearrange(flat), in0=gf, scalar=-1.0, in1=gf, op0=ALU.mult, op1=ALU.max
-            )
-            nc.vector.tensor_scalar(g_sgn[:].rearrange(flat), gf, 0.0, 2.0, op0=ALU.is_ge, op1=ALU.mult)
-            nc.vector.tensor_tensor(
-                out=g_bias[:].rearrange(flat), in0=g_abs[:].rearrange(flat), in1=bm_sb[:].rearrange(flat), op=ALU.mult
-            )
-            nc.vector.tensor_scalar_add(g_sgn[:].rearrange(flat), g_sgn[:].rearrange(flat), -1.0)
 
-        def perm_wm(k):
-            src = wm_raw[:].rearrange("p (k c t b) -> p k t c b", k=2, t=4, b=2)
+        def order_words(out, words):
             nc.vector.tensor_copy(
-                out=wm_cols[:, k, :, :].rearrange("p t (c b) -> p t c b", b=2), in_=src[:, k, :, :, :]
+                out=out.rearrange("p t (c b) -> p t c b", b=2), in_=words.rearrange("p (c t b) -> p t c b", t=4, b=2)
             )
 
-        def perm_wms():
+        def order_wm(k):
+            order_words(wm_cols[:, k, :, :], wm_raw[:, k, :])
+
+        def order_wm_scales():
             nc.vector.tensor_copy(
-                out=wms_cols[:], in_=wms_raw[:].rearrange("p (k c t) -> p k t c", k=2, t=4)
+                out=wm_scales_cols[:], in_=wm_scales_raw[:].rearrange("p k (c t) -> p k t c", t=4)
             )
 
-        def perm_w2(w, k):
-            nc.vector.tensor_copy(
-                out=w2_cols[:, w, k, :, :].rearrange("p t (c b) -> p t c b", b=2),
-                in_=w2_raw[:, w, k, :].rearrange("p (c t b) -> p t c b", t=4, b=2),
-            )
+        def order_w2(i):
+            if 0 <= i < 4:
+                w = i // 2
+                if i % 2 == 0:
+                    for k in range(KG):
+                        order_words(w2_cols[:, w, k, :, :], w2_raw[:, w, k, :])
+                else:
+                    nc.vector.tensor_copy(
+                        out=w2_scales_cols[:, w, :, :, :],
+                        in_=w2_scales_raw[:, w, :, :].rearrange("p k (c t) -> p k t c", t=4),
+                    )
 
-        def perm_w2s(w):
-            nc.vector.tensor_copy(
-                out=w2s_cols[:, w, :, :, :], in_=w2s_raw[:, w, :, :].rearrange("p k (c t) -> p k t c", t=4)
-            )
+        def prepare_gain():
+            nc.vector.tensor_scalar(g_sign[:], g_sb[:], 0.0, 2.0, op0=ALU.is_ge, op1=ALU.mult)
+            nc.vector.scalar_tensor_tensor(out=g_abs[:], in0=g_sb[:], scalar=-1.0, in1=g_sb[:], op0=ALU.mult, op1=ALU.max)
+            nc.vector.tensor_scalar_add(g_sign[:], g_sign[:], -1.0)
+            nc.vector.tensor_tensor(out=g_bias[:], in0=g_abs[:], in1=bm_sb[:], op=ALU.mult)
 
-        def m_turn(q, h):
-            pt = psum.tile([P, 2, 2, P], F32, name="pt", tag="pt", bufs=2)
-            for a in range(2):
-                words = m_raw[q][:, 2 * h + a, :].bitcast(F32)
-                for u in range(2):
-                    nc.tensor.transpose(pt[:, a, u, :], words[:, u : 2 * P : 2], ident[:])
-            if h == 0:
-                mg[q] = turn("mg", [P, R, 4], BF16, 2)
-            dst = mg[q][:, 256 * h : 256 * (h + 1), :].rearrange("p r t -> p (r t)").bitcast(F32)
-            nc.scalar.copy(
-                out=dst.rearrange("p (a r u) -> p a r u", a=2, u=2), in_=pt[:].rearrange("p a u r -> p a r u")
-            )
 
-        def m_quant(q):
-            mq[q] = turn("mq", [P, R], U32, 2)
-            ms[q] = turn("ms", [P, R], U8, 2)
-            nc.vector.quantize_mx(
-                out=mq[q][:].bitcast(FP8X4), scales=ms[q][:], in_=mg[q][:].rearrange("p r t -> p (r t)")
-            )
+        def quarter(i):
+            q, j = divmod(i, 4)
+            return (q, j) if 0 <= q < CHUNKS else (None, None)
 
-        def x_turn(q, h):
-            pt = psum.tile([P, 2, 2, P], F32, name="pt", tag="pt", bufs=2)
-            for a in range(2):
-                words = x_raw[q][:, 2 * h + a, :].bitcast(F32)
-                for u in range(2):
-                    nc.tensor.transpose(pt[:, a, u, :], words[:, u : 2 * P : 2], ident[:])
-            if h == 0:
-                xt[q] = turn("xt", [P, 2, R], F32, 4)
-            nc.scalar.copy(
-                out=xt[q][:, :, 256 * h : 256 * (h + 1)].rearrange("p u (a r) -> p u a r", a=2),
-                in_=pt[:].rearrange("p a u r -> p u a r"),
-            )
+        def turn_words(bank, i, rows, u):
+            nc.tensor.transpose(bank[:, i, :], rows.bitcast(F32)[:, u : 2 * P : 2], ident[:])
 
-        def x_of(q, t):
-            return xt[q][:, t // 2, :].bitcast(BF16)[:, t % 2 : 2 * R : 2]
+        def turn_m(i):
+            q, h = quarter(i)
+            if q is not None and h < 2:
+                m_turned[q, h] = turn_bank()
+                for a in range(2):
+                    for u in range(2):
+                        turn_words(m_turned[q, h], 2 * a + u, m_raw[q][:, 2 * h + a, :], u)
 
-        def x_stats(q, t):
-            nc.vector.bn_stats(out=stats[q // 2][:, t, q % 2, :], in_=x_of(q, t))
-
-        def x_aggr(b):
-            for t in range(4):
-                nc.vector.bn_aggr(out=mv[b][:, t, :], in_=stats[b][:, t, :, :].rearrange("p c k -> p (c k)"))
-            nc.gpsimd.tensor_scalar(rs[b][:], mv[b][:, :, 1], EPS, 1.0, op0=ALU.add, op1=ALU.mult)
-            nc.gpsimd.tensor_tensor(out=rs[b][:], in0=rs[b][:], in1=neg_half[:], op=ALU.pow)
-
-        def x_norm(q):
-            b = q // 2
-            xn[q] = turn("xn", [P, 4, R], F32, 4)
-            for t in range(4):
-                nc.vector.tensor_scalar(
-                    xn[q][:, t, :], x_of(q, t), mv[b][:, t, 0:1], rs[b][:, t : t + 1], op0=ALU.subtract, op1=ALU.mult
+        def take_m(i):
+            q, h = quarter(i)
+            if q is not None and h < 2:
+                if h == 0:
+                    m_grouped[q] = turn("m_grouped", [P, R, 4], BF16, 3)
+                words = m_grouped[q][:, HALVES[h], :].rearrange("p r t -> p (r t)").bitcast(F32)
+                nc.scalar.copy(
+                    out=words.rearrange("p (a r u) -> p a r u", a=2, u=2),
+                    in_=m_turned[q, h][:].rearrange("p (a u) r -> p a r u", u=2),
                 )
 
-        def stage1(q, j):
-            k = j // 2
-            for t in (2 * (j % 2), 2 * (j % 2) + 1):
-                ps = psum.tile([P, R], F32, name="ps1", tag="ps1", bufs=2)
-                nc.tensor.matmul_mx(
-                    out=ps[:], lhsT=wm_cols[:, k, t, :].bitcast(FP4X4), lhsT_scale=wms_cols[:, k, t, :],
-                    rhs=mq[q][:].bitcast(FP8X4), rhs_scale=ms[q][:], start=True, stop=True,
-                )
-                s1_ps[q, k, t] = ps
-
-        def relu(q, j):
-            k = j // 2
-            if j % 2 == 0:
-                planar[q, k] = turn("planar", [P, 4, R], BF16, 3)
-            for t in (2 * (j % 2), 2 * (j % 2) + 1):
-                nc.scalar.activation(
-                    out=planar[q, k][:, t, :], in_=s1_ps[q, k, t][:], func=ACT.Relu,
-                    scale=g_abs[:, k, t : t + 1], bias=g_bias[:, k, t : t + 1],
+        def quantize_m(i):
+            q, j = quarter(i)
+            if q is not None and j == 0:
+                m_codes[q] = turn("m_codes", [P, R], U32, 3)
+                m_scales[q] = turn("m_scales", [P, R], U8, 3)
+                nc.vector.quantize_mx(
+                    out=m_codes[q][:].bitcast(FP8X4), scales=m_scales[q][:],
+                    in_=m_grouped[q][:].rearrange("p r t -> p (r t)"),
                 )
 
-        def sign(q, j):
-            k = j // 2
-            for t in (2 * (j % 2), 2 * (j % 2) + 1):
-                nc.vector.tensor_scalar_mul(planar[q, k][:, t, :], planar[q, k][:, t, :], g_sgn[:, k, t : t + 1])
+        def hidden_slots(j):
+            return j // 2, (2 * (j % 2), 2 * (j % 2) + 1)
 
-        def interleave(q, k):
-            grouped[q, k] = turn("grouped", [P, R, 4], BF16, 2)
-            op = nc.scalar.copy if 2 * q + k in ACT_INTERLEAVE else nc.vector.tensor_copy
-            op(out=grouped[q, k][:], in_=planar[q, k][:].rearrange("p t r -> p r t"))
-
-        def a_quant(q, k):
-            aq[q, k] = turn("aq", [P, R], U32, 4)
-            asc[q, k] = turn("asc", [P, R], U8, 4)
-            nc.vector.quantize_mx(
-                out=aq[q, k][:].bitcast(FP8X4), scales=asc[q, k][:], in_=grouped[q, k][:].rearrange("p r t -> p (r t)")
-            )
-
-        def stage2(q, t):
-            for w, store in ((0, gam), (1, bet)):
-                ps = psum.tile([P, R], F32, name="ps2", tag="ps2", bufs=4)
-                for k in range(2):
+        def embed(i):
+            q, j = quarter(i)
+            if q is not None:
+                k, slots = hidden_slots(j)
+                for t in slots:
+                    h_bank[q, k, t] = embed_bank()
                     nc.tensor.matmul_mx(
-                        out=ps[:], lhsT=w2_cols[:, w, k, t, :].bitcast(FP4X4), lhsT_scale=w2s_cols[:, w, k, t, :],
-                        rhs=aq[q, k][:].bitcast(FP8X4), rhs_scale=asc[q, k][:], start=(k == 0), stop=(k == 1),
+                        out=h_bank[q, k, t][:],
+                        lhsT=wm_cols[:, k, t, :].bitcast(FP4X4), lhsT_scale=wm_scales_cols[:, k, t, :],
+                        rhs=m_codes[q][:].bitcast(FP8X4), rhs_scale=m_scales[q][:], start=True, stop=True,
                     )
-                store[q, t] = ps
 
-        def mod_u(q, t):
-            u_t[q, t] = turn("u", [P, R], F32, 3)
-            nc.vector.scalar_tensor_tensor(
-                out=u_t[q, t][:], in0=gam[q, t][:], scalar=1.0, in1=xn[q][:, t, :], op0=ALU.add, op1=ALU.mult
-            )
+        def rectify(i):
+            q, j = quarter(i)
+            if q is not None:
+                k, slots = hidden_slots(j)
+                if j % 2 == 0:
+                    a_planar[q, k] = turn("a_planar", [P, 4, R], BF16, 5)
+                for t in slots:
+                    nc.scalar.activation(
+                        out=a_planar[q, k][:, t, :], in_=h_bank[q, k, t][:], func=ACT.Relu,
+                        scale=g_abs[:, k, t : t + 1], bias=g_bias[:, k, t : t + 1],
+                    )
 
-        def mod_y(q, t):
-            y_t[q, t] = turn("y", [P, R], F32, 3)
-            nc.vector.tensor_tensor(out=y_t[q, t][:], in0=bet[q, t][:], in1=u_t[q, t][:], op=ALU.add)
+        def sign(i):
+            q, j = quarter(i)
+            if q is not None:
+                k, slots = hidden_slots(j)
+                for t in slots:
+                    part = a_planar[q, k][:, t, :]
+                    nc.vector.tensor_scalar_mul(part, part, g_sign[:, k, t : t + 1])
 
-        def mod_o(q, t):
-            if t == 0:
-                o_t[q] = turn("o", [P, 4, R], F32, 2)
-            yy = y_t[q, t][:]
-            nc.vector.scalar_tensor_tensor(out=o_t[q][:, t, :], in0=yy, scalar=0.2, in1=yy, op0=ALU.mult, op1=ALU.max)
+        def group_a(i):
+            q, j = quarter(i)
+            if q is not None:
+                k, h = j // 2, j % 2
+                if h == 0:
+                    a_grouped[q, k] = turn("a_grouped", [P, R, 4], BF16, 4)
+                copy = nc.scalar.copy if (q, k, h) in SCALAR_GROUPS else nc.vector.tensor_copy
+                copy(
+                    out=a_grouped[q, k][:, HALVES[h], :].rearrange("p (r i) t -> p r t i", i=4),
+                    in_=a_planar[q, k][:, :, HALVES[h]].rearrange("p t (r i) -> p r t i", i=4),
+                )
 
-        def out_turn(q, a):
-            pt = psum.tile([P, 4, P], F32, name="pt", tag="pt", bufs=2)
-            for t in range(4):
-                nc.tensor.transpose(pt[:, t, :], o_t[q][:, t, P * a : P * (a + 1)], ident[:])
-            orow = turn("orow", [P, P, 4], F32, 3)
-            nc.scalar.copy(out=orow[:], in_=pt[:].rearrange("r t p -> r p t"))
-            b, r0 = rows(q)
-            nc.sync.dma_start(
-                out=out_0[b, r0 + P * a : r0 + P * (a + 1), :], in_=orow[:].rearrange("r p t -> r (p t)")
-            )
+        def quantize_a(i):
+            q, j = quarter(i)
+            if q is not None and j % 2 == 0:
+                k = j // 2
+                a_codes[q, k] = turn("a_codes", [P, R], U32, 6)
+                a_scales[q, k] = turn("a_scales", [P, R], U8, 6)
+                nc.vector.quantize_mx(
+                    out=a_codes[q, k][:].bitcast(FP8X4), scales=a_scales[q, k][:],
+                    in_=a_grouped[q, k][:].rearrange("p r t -> p (r t)"),
+                )
 
-        def out_cast(q, h):
-            if h == 0:
-                ob[q] = turn("ob", [P, R, 4], BF16, 2)
-            nc.scalar.copy(
-                out=ob[q][:, 256 * h : 256 * (h + 1), :],
-                in_=o_t[q][:, :, 256 * h : 256 * (h + 1)].rearrange("p t r -> p r t"),
-            )
+        def turn_x_words(q, u):
+            bank = turn_bank()
+            for a in range(4):
+                turn_words(bank, a, x_raw[q][:, a, :], u)
+            return bank[:].rearrange("p a r -> p (a r)").bitcast(BF16)
 
-        def out_quant(q, h):
-            if h == 0:
-                oq[q] = turn("oq", [P, R], U32, 2)
-                osc[q] = turn("osc", [P, R], U8, 2)
-            part = slice(256 * h, 256 * (h + 1))
-            nc.vector.quantize_mx(
-                out=oq[q][:, part].bitcast(FP8X4), scales=osc[q][:, part],
-                in_=ob[q][:, part, :].rearrange("p r t -> p (r t)"),
-            )
-            c0 = q * R + 256 * h
-            nc.sync.dma_start(
-                out=out_1[0].rearrange("p n t -> p (n t)")[:, 4 * c0 : 4 * (c0 + 256)].bitcast(I32),
-                in_=oq[q][:, part].bitcast(I32),
-            )
-            if h == 1:
-                for Q in range(4):
+        STAT_PARTS = ((0, ((0, 0), (0, 1))), (1, ((1, 0), (1, 1))), (5, ((2, 0),)), (6, ((2, 1),)), (7, ((3, 0),)), (8, ((3, 1),)))
+
+        def stat_parts(i):
+            return dict(STAT_PARTS).get(i, ())
+
+        def turn_x_for_stats(i):
+            for q, u in stat_parts(i):
+                stat_bank[q, u] = turn_x_words(q, u)
+
+        def x_stats(i):
+            for q, u in stat_parts(i):
+                for h in range(2):
+                    nc.vector.bn_stats(
+                        out=stats[q // 2][:, u, 2 * (q % 2) + h, :], in_=stat_bank[q, u][:, R * h : R * (h + 1)]
+                    )
+
+        def sample_of(i):
+            return {0: 0, 7: 1}.get(i)
+
+        def x_spread(i):
+            b = sample_of(i)
+            if b is not None:
+                for t in range(4):
+                    part = stats[b][:, t // 2, :, 3 * (t % 2) : 3 * (t % 2) + 3]
+                    nc.vector.bn_aggr(out=mean_var[b][:, t, :], in_=part)
+                nc.vector.tensor_scalar_add(rstd[b][:], mean_var[b][:, :, 1], EPS)
+                nc.gpsimd.tensor_tensor(out=rstd[b][:], in0=rstd[b][:], in1=neg_half[:], op=ALU.pow)
+
+        def x_shift(i):
+            b = sample_of(i)
+            if b is not None:
+                nc.vector.scalar_tensor_tensor(
+                    out=shift[b][:], in0=mean_var[b][:, :, 0], scalar=-1.0, in1=rstd[b][:], op0=ALU.mult, op1=ALU.mult
+                )
+
+        def turn_x(i):
+            q, u = quarter(i)
+            if q is not None and u < 2:
+                x_bank[q, u] = turn_x_words(q, u)
+
+        def normalize_x(i):
+            q, u = quarter(i)
+            if q is not None and u < 2:
+                b = q // 2
+                if u == 0:
+                    xn[q] = turn("xn", [P, 4, R], F32, 3)
+                for e in range(2):
+                    t = 2 * u + e
+                    nc.scalar.activation(
+                        out=xn[q][:, t, :], in_=x_bank[q, u][:, e : 2 * R : 2], func=ACT.Identity,
+                        scale=rstd[b][:, t : t + 1], bias=shift[b][:, t : t + 1],
+                    )
+
+        def pieces(q, j):
+            if q == LAST:
+                return [(t, HALVES[j // 2]) for t in (2 * (j % 2), 2 * (j % 2) + 1)]
+            return [(j, slice(0, R))]
+
+        def project(i, w):
+            q, j = quarter(i)
+            if q is not None:
+                parts = pieces(q, j)
+                width = R // len(parts)
+                n = R if q < LAST else P
+                bank = map_bank(len(parts), width)
+                map_banks[w, q, j] = bank
+                for e, (t, cols) in enumerate(parts):
+                    for c in range(0, width, n):
+                        moving = slice(cols.start + c, cols.start + c + n)
+                        for k in range(KG):
+                            nc.tensor.matmul_mx(
+                                out=bank[:, e, c : c + n],
+                                lhsT=w2_cols[:, w, k, t, :].bitcast(FP4X4), lhsT_scale=w2_scales_cols[:, w, k, t, :],
+                                rhs=a_codes[q, k][:, moving].bitcast(FP8X4), rhs_scale=a_scales[q, k][:, moving],
+                                start=(k == 0), stop=(k == KG - 1),
+                            )
+
+        def scale_map(i):
+            project(i, 0)
+
+        def shift_map(i):
+            project(i, 1)
+
+        def modulate(i):
+            q, j = quarter(i)
+            if q is not None:
+                parts = pieces(q, j)
+                prod[q, j] = turn("prod", [P, len(parts), R // len(parts)], F32, 3)
+                for e, (t, cols) in enumerate(parts):
+                    nc.vector.scalar_tensor_tensor(
+                        out=prod[q, j][:, e, :], in0=map_banks[0, q, j][:, e, :], scalar=1.0, in1=xn[q][:, t, cols],
+                        op0=ALU.add, op1=ALU.mult,
+                    )
+
+        def add_shift(i):
+            q, j = quarter(i)
+            if q is not None:
+                parts = pieces(q, j)
+                y_tile[q, j] = turn("y", [P, len(parts), R // len(parts)], F32, 3)
+                for e in range(len(parts)):
+                    nc.vector.tensor_tensor(
+                        out=y_tile[q, j][:, e, :], in0=map_banks[1, q, j][:, e, :], in1=prod[q, j][:, e, :], op=ALU.add
+                    )
+
+        def leaky(i):
+            q, j = quarter(i)
+            if q is not None:
+                if j == 0:
+                    o_tile[q] = turn("o", [P, 4, R], F32, 3)
+                for e, (t, cols) in enumerate(pieces(q, j)):
+                    y = y_tile[q, j][:, e, :]
+                    nc.vector.scalar_tensor_tensor(
+                        out=o_tile[q][:, t, cols], in0=y, scalar=LEAK, in1=y, op0=ALU.mult, op1=ALU.max
+                    )
+
+        def turn_out(i):
+            q, a = quarter(i)
+            if q is not None:
+                o_turned[q, a] = turn_bank()
+                for t in range(4):
+                    nc.tensor.transpose(o_turned[q, a][:, t, :], o_tile[q][:, t, P * a : P * (a + 1)], ident[:])
+
+        def store_out(i):
+            q, a = quarter(i)
+            if q is not None:
+                rows = turn("rows", [P, P, 4], F32, 5)
+                nc.scalar.copy(out=rows[:], in_=o_turned[q, a][:].rearrange("r t p -> r p t"))
+                b, r0 = place(q)
+                nc.sync.dma_start(
+                    out=out_0[b, r0 + P * a : r0 + P * (a + 1), :], in_=rows[:].rearrange("r p t -> r (p t)")
+                )
+
+        def group_out(i):
+            q, h = quarter(i)
+            if q is not None and h < 2:
+                if h == 0:
+                    o_grouped[q] = turn("o_grouped", [P, R, 4], BF16, 3)
+                nc.scalar.copy(
+                    out=o_grouped[q][:, HALVES[h], :].rearrange("p (r i) t -> p r t i", i=4),
+                    in_=o_tile[q][:, :, HALVES[h]].rearrange("p t (r i) -> p r t i", i=4),
+                )
+
+        def quantize_out(i):
+            q, h = quarter(i)
+            if q is not None and h < 2:
+                if h == 0:
+                    o_codes[q] = turn("o_codes", [P, R], U32, 3)
+                nc.vector.quantize_mx(
+                    out=o_codes[q][:, HALVES[h]].bitcast(FP8X4), scales=o_scales[:, q, HALVES[h]],
+                    in_=o_grouped[q][:, HALVES[h], :].rearrange("p r t -> p (r t)"),
+                )
+                if q == LAST or h == 1:
+                    cols = HALVES[h] if q == LAST else slice(0, R)
+                    first, end = q * R + cols.start, q * R + cols.stop
                     nc.sync.dma_start(
-                        out=out_2[0, 4 * Q : 4 * Q + 4, q * R : (q + 1) * R].bitcast(I32),
-                        in_=osc[q][32 * Q : 32 * Q + 4, :].bitcast(I32),
+                        out=out_1[0].rearrange("p n t -> p (n t)")[:, 4 * first : 4 * end].bitcast(I32),
+                        in_=o_codes[q][:, cols].bitcast(I32),
                     )
+                b, r0 = place(q)
+                if r0 + R == POS and h == 1:
+                    for Q in range(4):
+                        nc.sync.dma_start(
+                            out=out_2[0, 4 * Q : 4 * Q + 4, b * POS : (b + 1) * POS].bitcast(I32),
+                            in_=o_scales[32 * Q : 32 * Q + 4, q - 1 : q + 1, :].rearrange("p k n -> p (k n)").bitcast(I32),
+                        )
+
+        STEPS = (
+            (order_w2, -8),
+            (group_out, 6),
+            (shift_map, -1),
+            (leaky, 1),
+            (turn_x, -3),
+            (add_shift, 0),
+            (modulate, -1),
+            (x_spread, -9),
+            (turn_out, 4),
+            (embed, -12),
+            (x_stats, -11),
+            (scale_map, -2),
+            (store_out, 5),
+            (sign, -10),
+            (group_a, -7),
+            (quantize_out, 9),
+            (quantize_a, -5),
+            (rectify, -12),
+            (turn_m, -18),
+            (take_m, -18),
+            (normalize_x, -3),
+            (quantize_m, -16),
+            (turn_x_for_stats, -12),
+            (x_shift, -7),
+        )
+        lags = [lag for step, lag in STEPS]
 
         with tc.manual_schedule():
-            perm_wms()
-            perm_wm(0)
-            prep_gain()
-            perm_wm(1)
-            for i in range(-8, 4 * NCH + 9):
-                qc, tcur = divmod(i, 4)
-                if 0 <= qc < NCH:
-                    stage2(qc, tcur)
-                qb, jb = divmod(i + 6, 4)
-                if 0 <= qb < NCH:
-                    stage1(qb, jb)
-                    relu(qb, jb)
-                if 0 <= qc < NCH:
-                    mod_u(qc, tcur)
-                qs, js = divmod(i + 5, 4)
-                if 0 <= qs < NCH:
-                    sign(qs, js)
-                if 0 <= qc < NCH:
-                    mod_y(qc, tcur)
-                if i % 2 == 0:
-                    qi, ki = divmod((i + 4) // 2, 2)
-                    if 0 <= qi < NCH:
-                        interleave(qi, ki)
-                else:
-                    qi, ki = divmod((i + 3) // 2, 2)
-                    if 0 <= qi < NCH:
-                        a_quant(qi, ki)
-                if i in (-4, -3):
-                    perm_w2s(i + 4)
-                if i in (-4, -3):
-                    perm_w2(0, i + 4)
-                if i in (-2, -1):
-                    perm_w2(1, i + 2)
-                qa, ha = divmod(i + 8, 4)
-                if 0 <= qa < NCH and ha < 2:
-                    m_turn(qa, ha)
-                    if ha == 1:
-                        m_quant(qa)
-                if i == -6:
-                    x_turn(0, 0)
-                    x_turn(0, 1)
-                if i == -5:
-                    x_turn(1, 0)
-                    x_turn(1, 1)
-                    for t in range(4):
-                        x_stats(0, t)
-                if i == -4:
-                    for t in range(4):
-                        x_stats(1, t)
-                    x_aggr(0)
-                if i == -3:
-                    x_norm(0)
-                if i == 0:
-                    x_norm(1)
-                if 0 <= i < 4:
-                    x_turn(2 + i // 2, i % 2)
-                if i in (2, 3, 4, 5):
-                    for t in (0, 1):
-                        x_stats(2 + (i - 2) // 2, 2 * (i % 2) + t)
-                if i == 5:
-                    x_aggr(1)
-                    x_norm(2)
-                if i == 7:
-                    x_norm(3)
-                if 0 <= qc < NCH:
-                    mod_o(qc, tcur)
-                qd, ad = divmod(i - 5, 4)
-                if 0 <= qd < NCH:
-                    out_turn(qd, ad)
-                    if ad < 2:
-                        out_cast(qd, ad)
-                    if ad in (1, 2):
-                        out_quant(qd, ad - 1)
+            order_wm(0)
+            order_wm_scales()
+            prepare_gain()
+            order_wm(1)
+            for i in range(min(lags), 4 * CHUNKS + max(lags)):
+                for step, lag in STEPS:
+                    step(i - lag)

from contextlib import ExitStack

import concourse.mybir as mybir
from concourse.masks import make_identity

B, POS, S, K, C = 2, 1024, 512, 1024, 512
FLOPS = 3 * 2 * B * POS * S * K

F32 = mybir.dt.float32
BF16 = mybir.dt.bfloat16
I32 = mybir.dt.int32
U32 = mybir.dt.uint32
U8 = mybir.dt.uint8
FP8X4 = mybir.dt.float8_e4m3fn_x4
FP4X4 = mybir.dt.float4_e2m1fn_x4
ACT = mybir.ActivationFunctionType
ALU = mybir.AluOpType

P = 128
R = 512
CHUNKS = B * POS // R
LAST = CHUNKS - 1
KG = K // 512
EPS = 1e-5
LEAK = 0.2
HALVES = (slice(0, R // 2), slice(R // 2, R))

SCALAR_GROUPS = (
    (0, 0, 0), (0, 0, 1), (0, 1, 1), (1, 0, 0), (1, 1, 1), (2, 0, 0), (2, 0, 1), (2, 1, 0), (3, 0, 0),
    (3, 0, 1), (3, 1, 0),
)


def tile_spademodulationpointwise_x2_kernel(
    tc, x, m, wm_words, wm_scales, bm, g, wg_words, wg_scales, wb_words, wb_scales, out_0, out_1, out_2
):
    nc = tc.nc
    with ExitStack() as ctx:
        keep = ctx.enter_context(tc.tile_pool(name="keep", bufs=1))
        work = ctx.enter_context(tc.tile_pool(name="work", bufs=2))
        psum = ctx.enter_context(tc.psum_pool(name="psum", bufs=2))

        def fixed(name, shape, dtype):
            return keep.tile(shape, dtype, name=name, tag=name, align_bytes=64)

        def turn(tag, shape, dtype, bufs):
            return work.tile(shape, dtype, name=tag, tag=tag, bufs=bufs, align_bytes=64)

        def embed_bank():
            return psum.tile([P, R], F32, name="embed", tag="embed", bufs=2)

        def map_bank(pieces, width):
            return psum.tile([P, pieces, width], F32, name="map", tag="map", bufs=3)

        def turn_bank():
            return psum.tile([P, 4, P], F32, name="turned", tag="turned", bufs=3)

        ident = fixed("ident", [P, P], F32)
        zero = fixed("zero", [P, 4], F32)
        neg_half = fixed("neg_half", [P, 4], F32)
        m_raw = [fixed("m_raw%d" % q, [P, 4, S], BF16) for q in range(CHUNKS)]
        x_raw = [fixed("x_raw%d" % q, [P, 4, C], BF16) for q in range(CHUNKS)]
        wm_raw = fixed("wm_raw", [P, KG, 2 * 512], U8)
        wm_cols = fixed("wm_cols", [P, KG, 4, 2 * P], U8)
        wm_scales_raw = fixed("wm_scales_raw", [P, KG, 512], U8)
        wm_scales_cols = fixed("wm_scales_cols", [P, KG, 4, P], U8)
        w2_raw = fixed("w2_raw", [P, 2, KG, 2 * C], U8)
        w2_cols = fixed("w2_cols", [P, 2, KG, 4, 2 * P], U8)
        w2_scales_raw = fixed("w2_scales_raw", [P, 2, KG, C], U8)
        w2_scales_cols = fixed("w2_scales_cols", [P, 2, KG, 4, P], U8)
        bm_sb = fixed("bm_sb", [P, KG, 4], BF16)
        g_sb = fixed("g_sb", [P, KG, 4], BF16)
        g_abs = fixed("g_abs", [P, KG, 4], F32)
        g_sign = fixed("g_sign", [P, KG, 4], F32)
        g_bias = fixed("g_bias", [P, KG, 4], F32)
        stats = [fixed("stats%d" % b, [P, 2, 4, 6], F32) for b in range(B)]
        mean_var = [fixed("mean_var%d" % b, [P, 4, 2], F32) for b in range(B)]
        rstd = [fixed("rstd%d" % b, [P, 4], F32) for b in range(B)]
        shift = [fixed("shift%d" % b, [P, 4], F32) for b in range(B)]

        o_scales = fixed("o_scales", [P, CHUNKS, R], U8)

        nc.vector.memset(wm_scales_raw[:].rearrange("p k n -> p (k n)").bitcast(I32), 0)
        nc.vector.memset(w2_scales_raw[:].rearrange("p w k n -> p (w k n)").bitcast(I32), 0)
        nc.vector.memset(zero[:], 0.0)
        make_identity(nc, ident[:])

        def place(q):
            return q // (POS // R), q % (POS // R) * R

        def load_m(q):
            b, r0 = place(q)
            for h in range(2):
                rows = m[b, r0 + 256 * h : r0 + 256 * (h + 1), :].rearrange("(a p) s -> p a s", p=P)
                nc.sync.dma_start(out=m_raw[q][:, 2 * h : 2 * h + 2, :], in_=rows)

        def load_x(q):
            b, r0 = place(q)
            nc.sync.dma_start(out=x_raw[q][:], in_=x[b, r0 : r0 + R, :].rearrange("(a p) c -> p a c", p=P))

        nc.sync.dma_start(out=wm_raw[:].rearrange("p k n -> p (k n)").bitcast(I32), in_=wm_words[0].bitcast(I32))
        load_m(0)
        for Q in range(4):
            nc.scalar.dma_start(
                out=wm_scales_raw[32 * Q : 32 * Q + 4, :, :].rearrange("p k n -> p (k n)").bitcast(I32),
                in_=wm_scales[0, 4 * Q : 4 * Q + 4, :].bitcast(I32),
            )
        nc.scalar.dma_start(out=g_sb[:], in_=g.rearrange("(k p t) -> p k t", p=P, t=4))
        nc.scalar.dma_start(out=bm_sb[:], in_=bm.rearrange("(k p t) -> p k t", p=P, t=4))
        nc.scalar.activation(out=neg_half[:], in_=zero[:], func=ACT.Identity, bias=-0.5, scale=1.0)
        load_m(1)
        load_x(0)
        load_x(1)
        for w, words in enumerate((wg_words, wb_words)):
            nc.sync.dma_start(out=w2_raw[:, w, :, :].bitcast(I32), in_=words.rearrange("k p n -> p k n").bitcast(I32))
        for w, scales in enumerate((wg_scales, wb_scales)):
            for Q in range(4):
                nc.sync.dma_start(
                    out=w2_scales_raw[32 * Q : 32 * Q + 4, w, :, :].bitcast(I32),
                    in_=scales[:, 4 * Q : 4 * Q + 4, :].rearrange("k q n -> q k n").bitcast(I32),
                )
        load_m(2)
        load_x(2)
        load_x(3)
        load_m(3)

        m_turned, m_grouped, m_codes, m_scales = {}, {}, {}, {}
        h_bank, a_planar, a_grouped, a_codes, a_scales = {}, {}, {}, {}, {}
        stat_bank, x_bank, xn, map_banks = {}, {}, {}, {}
        prod, y_tile, o_tile, o_turned = {}, {}, {}, {}
        o_grouped, o_codes = {}, {}


        def order_words(out, words):
            nc.vector.tensor_copy(
                out=out.rearrange("p t (c b) -> p t c b", b=2), in_=words.rearrange("p (c t b) -> p t c b", t=4, b=2)
            )

        def order_wm(k):
            order_words(wm_cols[:, k, :, :], wm_raw[:, k, :])

        def order_wm_scales():
            nc.vector.tensor_copy(
                out=wm_scales_cols[:], in_=wm_scales_raw[:].rearrange("p k (c t) -> p k t c", t=4)
            )

        def order_w2(i):
            if 0 <= i < 4:
                w = i // 2
                if i % 2 == 0:
                    for k in range(KG):
                        order_words(w2_cols[:, w, k, :, :], w2_raw[:, w, k, :])
                else:
                    nc.vector.tensor_copy(
                        out=w2_scales_cols[:, w, :, :, :],
                        in_=w2_scales_raw[:, w, :, :].rearrange("p k (c t) -> p k t c", t=4),
                    )

        def prepare_gain():
            nc.vector.tensor_scalar(g_sign[:], g_sb[:], 0.0, 2.0, op0=ALU.is_ge, op1=ALU.mult)
            nc.vector.scalar_tensor_tensor(out=g_abs[:], in0=g_sb[:], scalar=-1.0, in1=g_sb[:], op0=ALU.mult, op1=ALU.max)
            nc.vector.tensor_scalar_add(g_sign[:], g_sign[:], -1.0)
            nc.vector.tensor_tensor(out=g_bias[:], in0=g_abs[:], in1=bm_sb[:], op=ALU.mult)


        def quarter(i):
            q, j = divmod(i, 4)
            return (q, j) if 0 <= q < CHUNKS else (None, None)

        def turn_words(bank, i, rows, u):
            nc.tensor.transpose(bank[:, i, :], rows.bitcast(F32)[:, u : 2 * P : 2], ident[:])

        def turn_m(i):
            q, h = quarter(i)
            if q is not None and h < 2:
                m_turned[q, h] = turn_bank()
                for a in range(2):
                    for u in range(2):
                        turn_words(m_turned[q, h], 2 * a + u, m_raw[q][:, 2 * h + a, :], u)

        def take_m(i):
            q, h = quarter(i)
            if q is not None and h < 2:
                if h == 0:
                    m_grouped[q] = turn("m_grouped", [P, R, 4], BF16, 3)
                words = m_grouped[q][:, HALVES[h], :].rearrange("p r t -> p (r t)").bitcast(F32)
                nc.scalar.copy(
                    out=words.rearrange("p (a r u) -> p a r u", a=2, u=2),
                    in_=m_turned[q, h][:].rearrange("p (a u) r -> p a r u", u=2),
                )

        def quantize_m(i):
            q, j = quarter(i)
            if q is not None and j == 0:
                m_codes[q] = turn("m_codes", [P, R], U32, 3)
                m_scales[q] = turn("m_scales", [P, R], U8, 3)
                nc.vector.quantize_mx(
                    out=m_codes[q][:].bitcast(FP8X4), scales=m_scales[q][:],
                    in_=m_grouped[q][:].rearrange("p r t -> p (r t)"),
                )

        def hidden_slots(j):
            return j // 2, (2 * (j % 2), 2 * (j % 2) + 1)

        def embed(i):
            q, j = quarter(i)
            if q is not None:
                k, slots = hidden_slots(j)
                for t in slots:
                    h_bank[q, k, t] = embed_bank()
                    nc.tensor.matmul_mx(
                        out=h_bank[q, k, t][:],
                        lhsT=wm_cols[:, k, t, :].bitcast(FP4X4), lhsT_scale=wm_scales_cols[:, k, t, :],
                        rhs=m_codes[q][:].bitcast(FP8X4), rhs_scale=m_scales[q][:], start=True, stop=True,
                    )

        def rectify(i):
            q, j = quarter(i)
            if q is not None:
                k, slots = hidden_slots(j)
                if j % 2 == 0:
                    a_planar[q, k] = turn("a_planar", [P, 4, R], BF16, 5)
                for t in slots:
                    nc.scalar.activation(
                        out=a_planar[q, k][:, t, :], in_=h_bank[q, k, t][:], func=ACT.Relu,
                        scale=g_abs[:, k, t : t + 1], bias=g_bias[:, k, t : t + 1],
                    )

        def sign(i):
            q, j = quarter(i)
            if q is not None:
                k, slots = hidden_slots(j)
                for t in slots:
                    part = a_planar[q, k][:, t, :]
                    nc.vector.tensor_scalar_mul(part, part, g_sign[:, k, t : t + 1])

        def group_a(i):
            q, j = quarter(i)
            if q is not None:
                k, h = j // 2, j % 2
                if h == 0:
                    a_grouped[q, k] = turn("a_grouped", [P, R, 4], BF16, 4)
                copy = nc.scalar.copy if (q, k, h) in SCALAR_GROUPS else nc.vector.tensor_copy
                copy(
                    out=a_grouped[q, k][:, HALVES[h], :].rearrange("p (r i) t -> p r t i", i=4),
                    in_=a_planar[q, k][:, :, HALVES[h]].rearrange("p t (r i) -> p r t i", i=4),
                )

        def quantize_a(i):
            q, j = quarter(i)
            if q is not None and j % 2 == 0:
                k = j // 2
                a_codes[q, k] = turn("a_codes", [P, R], U32, 6)
                a_scales[q, k] = turn("a_scales", [P, R], U8, 6)
                nc.vector.quantize_mx(
                    out=a_codes[q, k][:].bitcast(FP8X4), scales=a_scales[q, k][:],
                    in_=a_grouped[q, k][:].rearrange("p r t -> p (r t)"),
                )

        def turn_x_words(q, u):
            bank = turn_bank()
            for a in range(4):
                turn_words(bank, a, x_raw[q][:, a, :], u)
            return bank[:].rearrange("p a r -> p (a r)").bitcast(BF16)

        STAT_PARTS = ((0, ((0, 0), (0, 1))), (1, ((1, 0), (1, 1))), (5, ((2, 0),)), (6, ((2, 1),)), (7, ((3, 0),)), (8, ((3, 1),)))

        def stat_parts(i):
            return dict(STAT_PARTS).get(i, ())

        def turn_x_for_stats(i):
            for q, u in stat_parts(i):
                stat_bank[q, u] = turn_x_words(q, u)

        def x_stats(i):
            for q, u in stat_parts(i):
                for h in range(2):
                    nc.vector.bn_stats(
                        out=stats[q // 2][:, u, 2 * (q % 2) + h, :], in_=stat_bank[q, u][:, R * h : R * (h + 1)]
                    )

        def sample_of(i):
            return {0: 0, 7: 1}.get(i)

        def x_spread(i):
            b = sample_of(i)
            if b is not None:
                for t in range(4):
                    part = stats[b][:, t // 2, :, 3 * (t % 2) : 3 * (t % 2) + 3]
                    nc.vector.bn_aggr(out=mean_var[b][:, t, :], in_=part)
                nc.vector.tensor_scalar_add(rstd[b][:], mean_var[b][:, :, 1], EPS)
                nc.gpsimd.tensor_tensor(out=rstd[b][:], in0=rstd[b][:], in1=neg_half[:], op=ALU.pow)

        def x_shift(i):
            b = sample_of(i)
            if b is not None:
                nc.vector.scalar_tensor_tensor(
                    out=shift[b][:], in0=mean_var[b][:, :, 0], scalar=-1.0, in1=rstd[b][:], op0=ALU.mult, op1=ALU.mult
                )

        def turn_x(i):
            q, u = quarter(i)
            if q is not None and u < 2:
                x_bank[q, u] = turn_x_words(q, u)

        def normalize_x(i):
            q, u = quarter(i)
            if q is not None and u < 2:
                b = q // 2
                if u == 0:
                    xn[q] = turn("xn", [P, 4, R], F32, 3)
                for e in range(2):
                    t = 2 * u + e
                    nc.scalar.activation(
                        out=xn[q][:, t, :], in_=x_bank[q, u][:, e : 2 * R : 2], func=ACT.Identity,
                        scale=rstd[b][:, t : t + 1], bias=shift[b][:, t : t + 1],
                    )

        def pieces(q, j):
            if q == LAST:
                return [(t, HALVES[j // 2]) for t in (2 * (j % 2), 2 * (j % 2) + 1)]
            return [(j, slice(0, R))]

        def project(i, w):
            q, j = quarter(i)
            if q is not None:
                parts = pieces(q, j)
                width = R // len(parts)
                n = R if q < LAST else P
                bank = map_bank(len(parts), width)
                map_banks[w, q, j] = bank
                for e, (t, cols) in enumerate(parts):
                    for c in range(0, width, n):
                        moving = slice(cols.start + c, cols.start + c + n)
                        for k in range(KG):
                            nc.tensor.matmul_mx(
                                out=bank[:, e, c : c + n],
                                lhsT=w2_cols[:, w, k, t, :].bitcast(FP4X4), lhsT_scale=w2_scales_cols[:, w, k, t, :],
                                rhs=a_codes[q, k][:, moving].bitcast(FP8X4), rhs_scale=a_scales[q, k][:, moving],
                                start=(k == 0), stop=(k == KG - 1),
                            )

        def scale_map(i):
            project(i, 0)

        def shift_map(i):
            project(i, 1)

        def modulate(i):
            q, j = quarter(i)
            if q is not None:
                parts = pieces(q, j)
                prod[q, j] = turn("prod", [P, len(parts), R // len(parts)], F32, 3)
                for e, (t, cols) in enumerate(parts):
                    nc.vector.scalar_tensor_tensor(
                        out=prod[q, j][:, e, :], in0=map_banks[0, q, j][:, e, :], scalar=1.0, in1=xn[q][:, t, cols],
                        op0=ALU.add, op1=ALU.mult,
                    )

        def add_shift(i):
            q, j = quarter(i)
            if q is not None:
                parts = pieces(q, j)
                y_tile[q, j] = turn("y", [P, len(parts), R // len(parts)], F32, 3)
                for e in range(len(parts)):
                    nc.vector.tensor_tensor(
                        out=y_tile[q, j][:, e, :], in0=map_banks[1, q, j][:, e, :], in1=prod[q, j][:, e, :], op=ALU.add
                    )

        def leaky(i):
            q, j = quarter(i)
            if q is not None:
                if j == 0:
                    o_tile[q] = turn("o", [P, 4, R], F32, 3)
                for e, (t, cols) in enumerate(pieces(q, j)):
                    y = y_tile[q, j][:, e, :]
                    nc.vector.scalar_tensor_tensor(
                        out=o_tile[q][:, t, cols], in0=y, scalar=LEAK, in1=y, op0=ALU.mult, op1=ALU.max
                    )

        def turn_out(i):
            q, a = quarter(i)
            if q is not None:
                o_turned[q, a] = turn_bank()
                for t in range(4):
                    nc.tensor.transpose(o_turned[q, a][:, t, :], o_tile[q][:, t, P * a : P * (a + 1)], ident[:])

        def store_out(i):
            q, a = quarter(i)
            if q is not None:
                rows = turn("rows", [P, P, 4], F32, 5)
                nc.scalar.copy(out=rows[:], in_=o_turned[q, a][:].rearrange("r t p -> r p t"))
                b, r0 = place(q)
                nc.sync.dma_start(
                    out=out_0[b, r0 + P * a : r0 + P * (a + 1), :], in_=rows[:].rearrange("r p t -> r (p t)")
                )

        def group_out(i):
            q, h = quarter(i)
            if q is not None and h < 2:
                if h == 0:
                    o_grouped[q] = turn("o_grouped", [P, R, 4], BF16, 3)
                nc.scalar.copy(
                    out=o_grouped[q][:, HALVES[h], :].rearrange("p (r i) t -> p r t i", i=4),
                    in_=o_tile[q][:, :, HALVES[h]].rearrange("p t (r i) -> p r t i", i=4),
                )

        def quantize_out(i):
            q, h = quarter(i)
            if q is not None and h < 2:
                if h == 0:
                    o_codes[q] = turn("o_codes", [P, R], U32, 3)
                nc.vector.quantize_mx(
                    out=o_codes[q][:, HALVES[h]].bitcast(FP8X4), scales=o_scales[:, q, HALVES[h]],
                    in_=o_grouped[q][:, HALVES[h], :].rearrange("p r t -> p (r t)"),
                )
                if q == LAST or h == 1:
                    cols = HALVES[h] if q == LAST else slice(0, R)
                    first, end = q * R + cols.start, q * R + cols.stop
                    nc.sync.dma_start(
                        out=out_1[0].rearrange("p n t -> p (n t)")[:, 4 * first : 4 * end].bitcast(I32),
                        in_=o_codes[q][:, cols].bitcast(I32),
                    )
                b, r0 = place(q)
                if r0 + R == POS and h == 1:
                    for Q in range(4):
                        nc.sync.dma_start(
                            out=out_2[0, 4 * Q : 4 * Q + 4, b * POS : (b + 1) * POS].bitcast(I32),
                            in_=o_scales[32 * Q : 32 * Q + 4, q - 1 : q + 1, :].rearrange("p k n -> p (k n)").bitcast(I32),
                        )

        STEPS = (
            (order_w2, -8),
            (group_out, 6),
            (shift_map, -1),
            (leaky, 1),
            (turn_x, -3),
            (add_shift, 0),
            (modulate, -1),
            (x_spread, -9),
            (turn_out, 4),
            (embed, -12),
            (x_stats, -11),
            (scale_map, -2),
            (store_out, 5),
            (sign, -10),
            (group_a, -7),
            (quantize_out, 9),
            (quantize_a, -5),
            (rectify, -12),
            (turn_m, -18),
            (take_m, -18),
            (normalize_x, -3),
            (quantize_m, -16),
            (turn_x_for_stats, -12),
            (x_shift, -7),
        )
        lags = [lag for step, lag in STEPS]

        with tc.manual_schedule():
            order_wm(0)
            order_wm_scales()
            prepare_gain()
            order_wm(1)
            for i in range(min(lags), 4 * CHUNKS + max(lags)):
                for step, lag in STEPS:
                    step(i - lag)
